import numpy as np
import ml_dtypes


def mxq(x, axis, fmt="e4m3"):
    dtype, down = {"e4m3": (ml_dtypes.float8_e4m3fn, 7), "e5m2": (ml_dtypes.float8_e5m2, 14)}[fmt]
    v = np.moveaxis(np.asarray(x, np.float32).astype(ml_dtypes.bfloat16).astype(np.float64), axis, -1)
    blocks = v.reshape(v.shape[:-1] + (-1, 32))
    amax = np.abs(blocks).max(-1, keepdims=True)
    byte = np.maximum(np.where(amax > 0, np.frexp(amax)[1] - 1 + 127, 0) - down, 1)
    scale = np.exp2(byte - 127.0)
    codes = (blocks / scale).astype(np.float32).astype(dtype).astype(np.float64)
    return np.moveaxis((codes * scale).reshape(v.shape), -1, axis)


WIDE = False


def mx_kscale(k):
    if not WIDE:
        return np.ones(k)
    levels = np.array([10, -10, 5, -5, 0])
    if k % 512:
        return np.exp2(np.random.permutation(np.resize(levels, k // 32))).repeat(32)
    a = np.empty((k // 512, 16))
    for p in range(k // 512):
        a[p, :8] = np.random.permutation(np.resize(levels, 8))
        for g in range(8):
            far = levels[np.abs(levels - a[p, g]) >= 10]
            a[p, g + 8] = far[np.random.randint(len(far))]
    return np.exp2(a.ravel()).repeat(32)


BF16 = ml_dtypes.bfloat16


def bf(x):
    return np.asarray(x, np.float32).astype(BF16)


def f64(x):
    return np.asarray(x).astype(np.float64)


E2M1 = np.array([0.0, 0.5, 1.0, 1.5, 2.0, 3.0, 4.0, 6.0, -0.0, -0.5, -1.0, -1.5, -2.0, -3.0, -4.0, -6.0])


def pack_weight(w, fmt):
    k, n = w.shape
    w = f64(bf(w)).reshape(k // 32, 32, n)
    amax = np.abs(w).max(1)
    if fmt == "e4m3":
        byte = np.frexp(amax)[1] - 1 + 127 - 7
    else:
        mant, ex = np.frexp(amax / 6.0)
        byte = np.where(mant > 0.5, ex, ex - 1) + 127
    byte = np.clip(np.where(amax > 0, byte, 1), 1, 254)
    scaled = (w * np.exp2(127.0 - byte)[:, None, :]).reshape(k, n).astype(np.float32)
    by_word = np.ascontiguousarray(scaled.reshape(k // 512, 128, 4, n).transpose(0, 1, 3, 2))
    if fmt == "e4m3":
        words = by_word.astype(ml_dtypes.float8_e4m3fn).view(np.uint8)
    else:
        c = by_word.astype(ml_dtypes.float4_e2m1fn).view(np.uint8) & 0xF
        words = c[..., 0::2] | (c[..., 1::2] << 4)
    return np.ascontiguousarray(words), np.ascontiguousarray(byte.astype(np.uint8).reshape(k // 512, 16, n))


def unpack_weight(words, scales, fmt):
    g, p, n, _ = words.shape
    if fmt == "e4m3":
        vals = np.ascontiguousarray(words).view(ml_dtypes.float8_e4m3fn).astype(np.float64)
    else:
        nib = np.empty((g, p, n, 4), np.uint8)
        nib[..., 0::2] = words & 0xF
        nib[..., 1::2] = words >> 4
        vals = E2M1[nib]
    vals = vals * np.repeat(np.exp2(scales.astype(np.float64) - 127.0), 8, axis=1)[..., None]
    return vals.transpose(0, 1, 3, 2).reshape(g * 512, n)
def pack4(w):
    words, scales = pack_weight(w, "e2m1")
    return words.reshape(words.shape[0], 128, -1), scales


def unpack4(words, scales):
    return unpack_weight(words.reshape(words.shape[0], 128, -1, 2), scales, "e2m1")


B, I, J, L = 1024, 1024, 1536, 512
KEEP, FRESH = 0.6, 0.8


def draw0():
    s, u = mx_kscale(B), mx_kscale(B)
    t = mx_kscale(J)
    h_free = np.random.standard_normal((B, I))
    v_free = np.random.standard_normal((B, J)) / np.sqrt(B)
    h_nudged = KEEP * h_free + FRESH * np.random.standard_normal((B, I))
    v_nudged = KEEP * v_free + FRESH * np.random.standard_normal((B, J)) / np.sqrt(B)
    v_free_words, v_free_scales = pack4(v_free / u[:, None] * t)
    proj_words, proj_scales = pack4(np.random.standard_normal((J, L)) / np.sqrt(J) / t[:, None])
    return {"h_nudged": bf(h_nudged * s[:, None]),
            "v_nudged": bf(v_nudged / s[:, None] * t),
            "h_free_neg": bf(-h_free * u[:, None]),
            "v_free_words": v_free_words, "v_free_scales": v_free_scales,
            "beta": bf(np.random.uniform(0.5, 1.0, J)),
            "velocity": bf(0.7 * np.random.standard_normal((I, J)) * t),
            "proj_words": proj_words, "proj_scales": proj_scales}


def core(h_nudged, v_nudged, h_free_neg, v_free_words, v_free_scales, beta, velocity, proj_words, proj_scales):
    hn = mxq(f64(h_nudged), 0, "e4m3")
    vn = mxq(f64(v_nudged), 0, "e4m3")
    hf = mxq(f64(h_free_neg), 0, "e4m3")
    vf = unpack4(v_free_words, v_free_scales)
    c = (hn.T @ vn) + (hf.T @ vf)
    d = c / f64(beta) + f64(velocity)
    return mxq(d, 1, "e4m3") @ unpack4(proj_words, proj_scales)


def e4m3fn_bytes(y):
    return np.clip(np.asarray(y, np.float64), -448.0, 448.0).astype(np.float32).astype(ml_dtypes.float8_e4m3fn).view(np.uint8)


def e4m3fn_values(b):
    return np.asarray(b, np.uint8).view(ml_dtypes.float8_e4m3fn).astype(np.float64)


def setup_inputs():
    d = draw0()
    x0 = np.asarray(d['h_nudged']).astype(np.float64)
    s = (np.max(np.abs(x0), axis=(1,), keepdims=True) / 448.0).astype(np.float32)
    out = {}
    for k, v in d.items():
        if k == 'h_nudged':
            out['h_nudged_bytes'] = e4m3fn_bytes(x0 / s.astype(np.float64))
            out['h_nudged_scale'] = s
        else:
            out[k] = v
    return out


def reference(h_nudged_bytes, h_nudged_scale, v_nudged, h_free_neg, v_free_words, v_free_scales, beta, velocity, proj_words, proj_scales):
    return core(e4m3fn_values(h_nudged_bytes) * h_nudged_scale.astype(np.float64), v_nudged, h_free_neg, v_free_words, v_free_scales, beta, velocity, proj_words, proj_scales)

@@ -1,0 +1,387 @@
+from contextlib import ExitStack
+
+import concourse.mybir as mybir
+from concourse.masks import make_identity
+
+B, I, J, L = 1024, 1024, 1536, 512
+FLOPS = 2 * 2 * B * I * J + 2 * I * J * L
+
+F32 = mybir.dt.float32
+BF16 = mybir.dt.bfloat16
+I32 = mybir.dt.int32
+U32 = mybir.dt.uint32
+U8 = mybir.dt.uint8
+FP8 = mybir.dt.float8_e4m3fn
+FP8X4 = mybir.dt.float8_e4m3fn_x4
+FP4X4 = mybir.dt.float4_e2m1fn_x4
+COPY = mybir.ActivationFunctionType.Copy
+MULT = mybir.AluOpType.mult
+ADD = mybir.AluOpType.add
+
+P = 128
+T = 4
+KP = P * T
+W = 512
+NG = J // KP
+NH = I // W
+NK = B // KP
+
+
+def tile_eqprop_projected_update_s3_kernel(
+    tc, h_nudged_bytes, h_nudged_scale, v_nudged, h_free_neg, v_free_words, v_free_scales,
+    beta, velocity, proj_words, proj_scales, out,
+):
+    nc = tc.nc
+    with ExitStack() as ctx:
+        keep = ctx.enter_context(tc.tile_pool(name="keep", bufs=1))
+        work = ctx.enter_context(tc.tile_pool(name="work", bufs=2))
+        psum = ctx.enter_context(tc.psum_pool(name="psum", bufs=1))
+
+        def kept(name, shape, dtype):
+            return keep.tile(shape, dtype, name=name, tag=name, align_bytes=64)
+
+        ident = kept("ident", [P, P], F32)
+        make_identity(nc, ident[:])
+        vfs_raw = kept("vfs_raw", [P, NK, J], U8)
+        prs = kept("prs", [P, NG, L], U8)
+        warm = kept("warm", [P, 1], F32)
+
+        hsc = kept("hsc", [P, NK, T], F32)
+        beta_sb = kept("beta_sb", [P, NG, T], BF16)
+        rbeta = kept("rbeta", [P, NG, T], F32)
+        hnb = [kept("hnb%d" % k, [P, T, I], U8) for k in range(NK)]
+        vfr = [kept("vfr%d" % k, [P, 2 * J], U8) for k in range(NK)]
+        vfp = [[kept("vfp%d%d" % (k, g), [P, 2 * KP], U8) for g in range(NG)] for k in range(NK)]
+        vfs = [kept("vfs%d" % g, [P, NK, KP], U8) for g in range(NG)]
+        hfr = [[kept("hfr%d%d" % (k, h), [P, T, W], BF16) for h in range(NH)] for k in range(NK)]
+        hnw = [[kept("hnw%d%d" % (k, h), [P, T, W], BF16) for h in range(NH)] for k in range(NK)]
+        vnr = [[kept("vnr%d%d" % (g, k), [P, T, KP], BF16) for k in range(NK)] for g in range(NG)]
+        vel = [[kept("vel%d%d" % (g, h), [P, T, KP], BF16) for h in range(NH)] for g in range(NG)]
+        hfc = [[kept("hfc%d%d" % (k, h), [P, W], U32) for h in range(NH)] for k in range(NK)]
+        hfs = [[kept("hfs%d%d" % (k, h), [P, W], U8) for h in range(NH)] for k in range(NK)]
+        hnc = [[kept("hnc%d%d" % (k, h), [P, W], U32) for h in range(NH)] for k in range(NK)]
+        hns = [[kept("hns%d%d" % (k, h), [P, W], U8) for h in range(NH)] for k in range(NK)]
+        vnc = [[kept("vnc%d%d" % (g, k), [P, KP], U32) for k in range(NK)] for g in range(NG)]
+        vns = [[kept("vns%d%d" % (g, k), [P, KP], U8) for k in range(NK)] for g in range(NG)]
+        dc = [[kept("dc%d%d" % (g, h), [P, W], U32) for h in range(NH)] for g in range(NG)]
+        ds = [[kept("ds%d%d" % (g, h), [P, W], U8) for h in range(NH)] for g in range(NG)]
+        prw = kept("prw", [P, NG, 2 * L], U8)
+
+        nc.vector.memset(vfs_raw[:].rearrange("p k n -> p (k n)").bitcast(I32), 0)
+        nc.vector.memset(warm[:], 0.0)
+        nc.gpsimd.memset(prs[:].rearrange("p g n -> p (g n)").bitcast(I32), 0)
+
+        ctx.enter_context(tc.manual_schedule())
+
+        hn_v = h_nudged_bytes.rearrange("(k p t) n -> k p t n", p=P, t=T)
+        hf_v = h_free_neg.rearrange("(k p t) n -> k p t n", p=P, t=T)
+        vn_v = v_nudged.rearrange("(k p t) n -> k p t n", p=P, t=T)
+        vel_v = velocity.rearrange("(h a p) n -> h p a n", p=P, a=T)
+
+        nc.scalar.dma_start(out=hsc[:], in_=h_nudged_scale.rearrange("(k p t) o -> p k (t o)", p=P, t=T))
+        nc.scalar.dma_start(out=beta_sb[:], in_=beta.rearrange("(g p t) -> p g t", p=P, t=T))
+        nc.scalar.activation(out=warm[:], in_=warm[:], func=COPY, scale=1.0)
+
+        def load_hf(k, h):
+            nc.sync.dma_start(out=hfr[k][h][:], in_=hf_v[k][:, :, h * W:(h + 1) * W])
+
+        def load_hn(k):
+            nc.sync.dma_start(out=hnb[k][:], in_=hn_v[k])
+
+        def load_vn(g):
+            for k in range(NK):
+                nc.sync.dma_start(out=vnr[g][k][:], in_=vn_v[k][:, :, g * KP:(g + 1) * KP])
+
+        def load_vel(g, h):
+            nc.sync.dma_start(out=vel[g][h][:], in_=vel_v[h][:, :, g * KP:(g + 1) * KP])
+
+        load_hn(0)
+        load_hf(0, 0)
+        for q in range(T):
+            nc.sync.dma_start(
+                out=vfs_raw[32 * q:32 * q + 4].bitcast(I32),
+                in_=v_free_scales[:, 4 * q:4 * q + 4, :].rearrange("k q n -> q k n").bitcast(I32),
+            )
+        for k in range(NK):
+            nc.sync.dma_start(out=vfr[k][:], in_=v_free_words[k])
+        load_hf(1, 0)
+        load_vn(0)
+        load_hn(1)
+        load_vel(0, 0)
+        load_vn(1)
+        load_vel(1, 0)
+        load_vn(2)
+        load_hf(0, 1)
+        load_vel(2, 0)
+        load_hf(1, 1)
+        nc.sync.dma_start(out=prw[:], in_=proj_words.rearrange("g p n -> p g n"))
+        for q in range(T):
+            nc.sync.dma_start(
+                out=prs[32 * q:32 * q + 4].bitcast(I32),
+                in_=proj_scales[:, 4 * q:4 * q + 4, :].rearrange("g q n -> q g n").bitcast(I32),
+            )
+        for g in range(NG):
+            load_vel(g, 1)
+
+        def widen(k, h):
+            for t in range(T):
+                nc.scalar.activation(
+                    out=hnw[k][h][:, t, :],
+                    in_=hnb[k][:, t, h * W:(h + 1) * W].bitcast(FP8),
+                    func=COPY,
+                    scale=hsc[:, k, t:t + 1],
+                )
+
+        def copy_on(engine, dst, src):
+            if engine == "v":
+                nc.vector.tensor_copy(out=dst, in_=src)
+            elif engine == "s":
+                nc.scalar.copy(out=dst, in_=src)
+            else:
+                nc.gpsimd.tensor_scalar(out=dst, in0=src, scalar1=1.0, scalar2=0.0, op0=MULT, op1=ADD)
+
+        grouped = {}
+
+        def new_grouped(key):
+            if key not in grouped:
+                grouped[key] = work.tile([P, W * T], BF16, name="grouped", tag="grouped", bufs=6, align_bytes=64)
+            return grouped[key]
+
+        def ilv_h(engine, key, raw, lo, hi):
+            x = new_grouped(key)
+            copy_on(engine, x[:].rearrange("p (n t) -> p n t", t=T)[:, lo:hi, :], raw[:].rearrange("p t n -> p n t")[:, lo:hi, :])
+
+        def ilv_v(engine, g, k, lo=0, hi=T):
+            x = new_grouped(("v", g, k))
+            copy_on(
+                engine,
+                x[:].rearrange("p (t m j) -> p t m j", t=T, j=T)[:, lo:hi],
+                vnr[g][k][:].rearrange("p j (m t) -> p t m j", t=T)[:, lo:hi],
+            )
+
+        def hf_ilv(engine, k, h, lo=0, hi=W):
+            ilv_h(engine, ("f", k, h), hfr[k][h], lo, hi)
+
+        def hn_ilv(engine, k, h, lo=0, hi=W):
+            ilv_h(engine, ("n", k, h), hnw[k][h], lo, hi)
+
+        def quant(key, codes, scales):
+            nc.vector.quantize_mx(out=codes[:].bitcast(FP8X4), scales=scales[:], in_=grouped[key][:])
+
+        def q_hf(k, h):
+            quant(("f", k, h), hfc[k][h], hfs[k][h])
+
+        def q_hn(k, h):
+            quant(("n", k, h), hnc[k][h], hns[k][h])
+
+        def q_v(g, k):
+            quant(("v", g, k), vnc[g][k], vns[g][k])
+
+        def perm_words(k, g):
+            nc.vector.tensor_copy(
+                out=vfp[k][g][:].rearrange("p (t m b) -> p t m b", t=T, b=2),
+                in_=vfr[k][:, 2 * KP * g:2 * KP * (g + 1)].rearrange("p (m t b) -> p t m b", t=T, b=2),
+            )
+
+        def perm_scales(g):
+            nc.vector.tensor_copy(
+                out=vfs[g][:].rearrange("p k (t m) -> p k t m", t=T),
+                in_=vfs_raw[:, :, KP * g:KP * (g + 1)].rearrange("p k (m t) -> p k t m", t=T),
+            )
+
+        def banks():
+            return [psum.tile([P, W], F32, name="c%d" % t, tag="c%d" % t) for t in range(T)]
+
+        def mm(cb, g, h, t, step):
+            cols = slice(t * P, (t + 1) * P)
+            k = step % NK
+            if step < NK:
+                lhsT = vfp[k][g][:, 2 * t * P:2 * (t + 1) * P].bitcast(FP4X4)
+                ls = vfs[g][:, k, cols]
+                rhs, rs = hfc[k][h], hfs[k][h]
+            else:
+                lhsT = vnc[g][k][:, cols].bitcast(FP8X4)
+                ls = vns[g][k][:, cols]
+                rhs, rs = hnc[k][h], hns[k][h]
+            nc.tensor.matmul_mx(
+                out=cb[t][:], lhsT=lhsT, lhsT_scale=ls, rhs=rhs[:].bitcast(FP8X4), rhs_scale=rs[:],
+                start=(step == 0), stop=(step == 2 * NK - 1),
+            )
+
+        def vel_t(g, h):
+            res = []
+            for c in range(2):
+                x = psum.tile([P, 2, 256], F32, name="vt", tag="vt", bufs=2)
+                for b in range(2):
+                    words = vel[g][h][:, 2 * c + b, :].bitcast(F32)
+                    for u in range(2):
+                        nc.tensor.transpose(x[:, u, b * P:(b + 1) * P], words[:, u:256:2], ident[:])
+                res.append(x)
+            return res
+
+        def drain(cb, g):
+            x = work.tile([P, T, W], F32, name="csc", tag="csc", bufs=2)
+            for t in range(T):
+                nc.scalar.activation(out=x[:, t, :], in_=cb[t][:], func=COPY, scale=rbeta[:, g, t:t + 1])
+            return x
+
+        def d_add(x, vt, c, dst):
+            nc.vector.tensor_tensor(
+                out=dst[:, 1024 * c:1024 * (c + 1)].rearrange("p (r u e) -> p r u e", u=2, e=2),
+                in0=x[:, :, 256 * c:256 * (c + 1)].rearrange("p (u e) r -> p r u e", e=2),
+                in1=vt[c][:].bitcast(BF16).rearrange("p u (r e) -> p r u e", e=2),
+                op=ADD,
+            )
+
+        def d_quant(g, h, dst, lo, hi):
+            nc.vector.quantize_mx(
+                out=dc[g][h][:, lo:hi].bitcast(FP8X4), scales=ds[g][h][:, lo:hi], in_=dst[:, T * lo:T * hi])
+
+        def d_tile():
+            return work.tile([P, W * T], BF16, name="dbf", tag="dbf", bufs=2, align_bytes=64)
+
+        def out_mm(bank, h, a, g):
+            cols = slice(a * P, (a + 1) * P)
+            nc.tensor.matmul_mx(
+                out=bank[:], lhsT=dc[g][h][:, cols].bitcast(FP8X4), lhsT_scale=ds[g][h][:, cols],
+                rhs=prw[:, g, :].bitcast(FP4X4), rhs_scale=prs[:, g, :], start=(g == 0), stop=(g == NG - 1))
+
+        def out_bank():
+            return psum.tile([P, L], F32, name="ob", tag="ob", bufs=2)
+
+        def store(bank, h, a, engine):
+            x = work.tile([P, L], F32, name="res", tag="res", bufs=4)
+            if engine == "s":
+                nc.scalar.copy(out=x[:], in_=bank[:])
+            else:
+                nc.vector.tensor_copy(out=x[:], in_=bank[:])
+            r = (h * T + a) * P
+            nc.sync.dma_start(out=out[r:r + P, :], in_=x[:])
+
+        hf_ilv("v", 0, 0)
+        perm_words(0, 0)
+        perm_scales(0)
+        q_hf(0, 0)
+        c1 = banks()
+        for t in range(T):
+            mm(c1, 0, 0, t, 0)
+        widen(0, 0)
+        perm_words(1, 0)
+        hf_ilv("v", 1, 0)
+        hn_ilv("s", 0, 0, 256, W)
+        ilv_v("v", 0, 0)
+        q_hf(1, 0)
+        for t in range(T):
+            mm(c1, 0, 0, t, 1)
+        widen(1, 0)
+        hn_ilv("v", 0, 0, 0, 256)
+        q_v(0, 0)
+        ilv_v("v", 0, 1, 0, 2)
+        q_hn(0, 0)
+        vt1 = vel_t(0, 0)
+        for t in range(T):
+            mm(c1, 0, 0, t, 2)
+        ilv_v("s", 0, 1, 2, T)
+        hn_ilv("v", 1, 0)
+        nc.vector.reciprocal(out=rbeta[:].rearrange("p g t -> p (g t)"), in_=beta_sb[:].rearrange("p g t -> p (g t)"))
+        q_v(0, 1)
+        q_hn(1, 0)
+        for t in range(T):
+            mm(c1, 0, 0, t, 3)
+
+        perm_words(0, 1)
+        ilv_v("s", 1, 0, 2, T)
+        ilv_v("v", 1, 0, 0, 2)
+        perm_words(1, 1)
+        perm_scales(1)
+        q_v(1, 0)
+        ilv_v("v", 1, 1)
+        perm_words(0, 2)
+        q_v(1, 1)
+
+        x1 = drain(c1, 0)
+
+        def unit(g, h, extra=()):
+            cb = banks()
+            vt = None
+            for t in range(T):
+                for step in range(2 * NK):
+                    mm(cb, g, h, t, step)
+                if t == 2:
+                    vt = vel_t(g, h)
+            return cb, vt
+
+        def d_step(x, vt, g, h):
+            dst = d_tile()
+            d_add(x, vt, 0, dst)
+            d_add(x, vt, 1, dst)
+            return dst
+
+        d1 = d_step(x1, vt1, 0, 0)
+        c2, vt2 = unit(1, 0)
+        hf_ilv("g", 0, 1)
+        ilv_v("s", 2, 1)
+        ilv_v("v", 2, 0)
+        d_quant(0, 0, d1, 0, W)
+        perm_words(1, 2)
+        perm_scales(2)
+        q_v(2, 0)
+        widen(0, 1)
+        q_v(2, 1)
+
+        x2 = drain(c2, 1)
+        hf_ilv("v", 1, 1)
+        q_hf(0, 1)
+        d2 = d_step(x2, vt2, 1, 0)
+        c3, vt3 = unit(2, 0)
+        widen(1, 1)
+        q_hf(1, 1)
+        hn_ilv("v", 0, 1)
+        d_quant(1, 0, d2, 0, W)
+        hn_ilv("s", 1, 1, 256, W)
+        hn_ilv("v", 1, 1, 0, 256)
+        q_hn(0, 1)
+
+        x3 = drain(c3, 2)
+        q_hn(1, 1)
+        d3 = d_step(x3, vt3, 2, 0)
+        d_quant(2, 0, d3, 0, W)
+        c4, vt4 = unit(0, 1)
+
+        x4 = drain(c4, 0)
+        d4 = d_step(x4, vt4, 0, 1)
+        d_quant(0, 1, d4, 0, W)
+        for a in range(2):
+            ob = out_bank()
+            for g in range(NG):
+                out_mm(ob, 0, a, g)
+            store(ob, 0, a, "s" if a else "v")
+        c5, vt5 = unit(1, 1)
+
+        x5 = drain(c5, 1)
+        d5 = d_step(x5, vt5, 1, 1)
+        d_quant(1, 1, d5, 0, W)
+        c6, vt6 = unit(2, 1)
+
+        obs = []
+        for a in range(2, T):
+            ob = out_bank()
+            for g in range(NG):
+                out_mm(ob, 0, a, g)
+            obs.append(ob)
+        x6 = drain(c6, 2)
+        store(obs[0], 0, 2, "v")
+        store(obs[1], 0, 3, "s")
+        last = [psum.tile([P, L], F32, name="c%d" % a, tag="c%d" % a) for a in range(T)]
+        for a in range(T):
+            for g in range(2):
+                out_mm(last[a], 1, a, g)
+        d6 = d_tile()
+        d_add(x6, vt6, 0, d6)
+        d_quant(2, 1, d6, 0, 256)
+        d_add(x6, vt6, 1, d6)
+        d_quant(2, 1, d6, 256, W)
+        for a in range(T):
+            out_mm(last[a], 1, a, 2)
+        for a in range(T):
+            store(last[a], 1, a, "s" if a % 2 == 0 else "v")

@@ -82,306 +82,360 @@ def tile_eqprop_projected_update_s3_kernel(
         nc.scalar.dma_start(out=beta_sb[:], in_=beta.rearrange("(g p t) -> p g t", p=P, t=T))
         nc.scalar.activation(out=warm[:], in_=warm[:], func=COPY, scale=1.0)
 
-        def load_hf(k, h):
-            nc.sync.dma_start(out=hfr[k][h][:], in_=hf_v[k][:, :, h * W:(h + 1) * W])
 
-        def load_hn(k):
-            nc.sync.dma_start(out=hnb[k][:], in_=hn_v[k])
-
-        def load_vn(g):
-            for k in range(NK):
+        def ld(what, *ix):
+            if what == "hf":
+                k, h = ix
+                nc.sync.dma_start(out=hfr[k][h][:], in_=hf_v[k][:, :, h * W:(h + 1) * W])
+            elif what == "hn":
+                nc.sync.dma_start(out=hnb[ix[0]][:], in_=hn_v[ix[0]])
+            elif what == "vn":
+                g, k = ix
                 nc.sync.dma_start(out=vnr[g][k][:], in_=vn_v[k][:, :, g * KP:(g + 1) * KP])
-
-        def load_vel(g, h):
-            nc.sync.dma_start(out=vel[g][h][:], in_=vel_v[h][:, :, g * KP:(g + 1) * KP])
-
-        load_hn(0)
-        load_hf(0, 0)
-        for q in range(T):
-            nc.sync.dma_start(
-                out=vfs_raw[32 * q:32 * q + 4].bitcast(I32),
-                in_=v_free_scales[:, 4 * q:4 * q + 4, :].rearrange("k q n -> q k n").bitcast(I32),
-            )
-        for k in range(NK):
-            nc.sync.dma_start(out=vfr[k][:], in_=v_free_words[k])
-        load_hf(1, 0)
-        load_vn(0)
-        load_hn(1)
-        load_vel(0, 0)
-        load_vn(1)
-        load_vel(1, 0)
-        load_vn(2)
-        load_hf(0, 1)
-        load_vel(2, 0)
-        load_hf(1, 1)
-        nc.sync.dma_start(out=prw[:], in_=proj_words.rearrange("g p n -> p g n"))
-        for q in range(T):
-            nc.sync.dma_start(
-                out=prs[32 * q:32 * q + 4].bitcast(I32),
-                in_=proj_scales[:, 4 * q:4 * q + 4, :].rearrange("g q n -> q g n").bitcast(I32),
-            )
-        for g in range(NG):
-            load_vel(g, 1)
-
-        def widen(k, h):
-            for t in range(T):
-                nc.scalar.activation(
-                    out=hnw[k][h][:, t, :],
-                    in_=hnb[k][:, t, h * W:(h + 1) * W].bitcast(FP8),
-                    func=COPY,
-                    scale=hsc[:, k, t:t + 1],
-                )
-
-        def copy_on(engine, dst, src):
-            if engine == "v":
-                nc.vector.tensor_copy(out=dst, in_=src)
-            elif engine == "s":
-                nc.scalar.copy(out=dst, in_=src)
+            elif what == "vel":
+                g, h = ix
+                nc.sync.dma_start(out=vel[g][h][:], in_=vel_v[h][:, :, g * KP:(g + 1) * KP])
+            elif what == "vfw":
+                nc.sync.dma_start(out=vfr[ix[0]][:], in_=v_free_words[ix[0]])
+            elif what == "prw":
+                nc.sync.dma_start(out=prw[:], in_=proj_words.rearrange("g p n -> p g n"))
             else:
-                nc.gpsimd.tensor_scalar(out=dst, in0=src, scalar1=1.0, scalar2=0.0, op0=MULT, op1=ADD)
+                dst, src = (vfs_raw, v_free_scales) if what == "vfs" else (prs, proj_scales)
+                for q4 in range(T):
+                    nc.sync.dma_start(
+                        out=dst[32 * q4:32 * q4 + 4].bitcast(I32),
+                        in_=src[:, 4 * q4:4 * q4 + 4, :].rearrange("g q n -> q g n").bitcast(I32),
+                    )
+
+        raws, codes, scales = {}, {}, {}
+        for k in range(NK):
+            for h in range(NH):
+                raws["f", k, h], codes["f", k, h], scales["f", k, h] = hfr[k][h], hfc[k][h], hfs[k][h]
+                raws["n", k, h], codes["n", k, h], scales["n", k, h] = hnw[k][h], hnc[k][h], hns[k][h]
+            for g in range(NG):
+                raws["v", g, k], codes["v", g, k], scales["v", g, k] = vnr[g][k], vnc[g][k], vns[g][k]
+
+        def part(pt):
+            return slice(0, W) if pt == 2 else slice(256 * pt, 256 * (pt + 1))
+
+        def wid(k, h, pt, e):
+            lo = part(pt).start
+            hi = part(pt).stop
+            for t in range(T):
+                src = hnb[k][:, t, h * W + lo:h * W + hi].bitcast(FP8)
+                if e == "S":
+                    nc.scalar.activation(out=hnw[k][h][:, t, lo:hi], in_=src, func=COPY, scale=hsc[:, k, t:t + 1])
+                else:
+                    nc.vector.tensor_scalar(
+                        out=hnw[k][h][:, t, lo:hi], in0=src, scalar1=hsc[:, k, t:t + 1], scalar2=None, op0=MULT)
+
+        def copy_on(e, dst, src):
+            if e == "V":
+                nc.vector.tensor_copy(out=dst, in_=src)
+            else:
+                nc.scalar.copy(out=dst, in_=src)
 
         grouped = {}
 
         def new_grouped(key):
             if key not in grouped:
-                grouped[key] = work.tile([P, W * T], BF16, name="grouped", tag="grouped", bufs=6, align_bytes=64)
+                grouped[key] = work.tile([P, W * T], BF16, name="grouped", tag="grouped", bufs=8, align_bytes=64)
             return grouped[key]
 
-        def ilv_h(engine, key, raw, lo, hi):
-            x = new_grouped(key)
-            copy_on(engine, x[:].rearrange("p (n t) -> p n t", t=T)[:, lo:hi, :], raw[:].rearrange("p t n -> p n t")[:, lo:hi, :])
+        def ilv(key, b, e):
+            dst = new_grouped(key)[:, 1024 * b:1024 * (b + 1)]
+            src = raws[key]
+            if key[0] == "v":
+                copy_on(
+                    e,
+                    dst.rearrange("p (t m j) -> p m j t", t=2, j=T),
+                    src[:].rearrange("p j (m t) -> p m j t", t=T)[:, :, :, 2 * b:2 * b + 2],
+                )
+            else:
+                copy_on(
+                    e,
+                    dst.rearrange("p (c i t) -> p c t i", i=4, t=T),
+                    src[:, :, 256 * b:256 * (b + 1)].rearrange("p t (c i) -> p c t i", i=4),
+                )
 
-        def ilv_v(engine, g, k, lo=0, hi=T):
-            x = new_grouped(("v", g, k))
-            copy_on(
-                engine,
-                x[:].rearrange("p (t m j) -> p t m j", t=T, j=T)[:, lo:hi],
-                vnr[g][k][:].rearrange("p j (m t) -> p t m j", t=T)[:, lo:hi],
-            )
+        def q(key, pt):
+            s = part(pt)
+            nc.vector.quantize_mx(
+                out=codes[key][:, s].bitcast(FP8X4), scales=scales[key][:, s], in_=grouped[key][:, T * s.start:T * s.stop])
 
-        def hf_ilv(engine, k, h, lo=0, hi=W):
-            ilv_h(engine, ("f", k, h), hfr[k][h], lo, hi)
-
-        def hn_ilv(engine, k, h, lo=0, hi=W):
-            ilv_h(engine, ("n", k, h), hnw[k][h], lo, hi)
-
-        def quant(key, codes, scales):
-            nc.vector.quantize_mx(out=codes[:].bitcast(FP8X4), scales=scales[:], in_=grouped[key][:])
-
-        def q_hf(k, h):
-            quant(("f", k, h), hfc[k][h], hfs[k][h])
-
-        def q_hn(k, h):
-            quant(("n", k, h), hnc[k][h], hns[k][h])
-
-        def q_v(g, k):
-            quant(("v", g, k), vnc[g][k], vns[g][k])
-
-        def perm_words(k, g):
+        def pw(k, g):
             nc.vector.tensor_copy(
                 out=vfp[k][g][:].rearrange("p (t m b) -> p t m b", t=T, b=2),
                 in_=vfr[k][:, 2 * KP * g:2 * KP * (g + 1)].rearrange("p (m t b) -> p t m b", t=T, b=2),
             )
 
-        def perm_scales(g):
+        def ps(g):
             nc.vector.tensor_copy(
                 out=vfs[g][:].rearrange("p k (t m) -> p k t m", t=T),
                 in_=vfs_raw[:, :, KP * g:KP * (g + 1)].rearrange("p k (m t) -> p k t m", t=T),
             )
 
-        def banks():
-            return [psum.tile([P, W], F32, name="c%d" % t, tag="c%d" % t) for t in range(T)]
+        def rb():
+            nc.vector.reciprocal(out=rbeta[:].rearrange("p g t -> p (g t)"), in_=beta_sb[:].rearrange("p g t -> p (g t)"))
 
-        def mm(cb, g, h, t, step):
+        acc, vts, cscs, dbfs, obs = {}, {}, {}, {}, {}
+
+        def bank(b, shape, dtype):
+            return psum.tile(shape, dtype, name="bank%d" % b, tag="bank%d" % b)
+
+        def mm(g, h, t, s0, s1, b=None):
+            if s0 == 0:
+                acc[g, h, t] = bank(b, [P, W], F32)
             cols = slice(t * P, (t + 1) * P)
-            k = step % NK
-            if step < NK:
-                lhsT = vfp[k][g][:, 2 * t * P:2 * (t + 1) * P].bitcast(FP4X4)
-                ls = vfs[g][:, k, cols]
-                rhs, rs = hfc[k][h], hfs[k][h]
+            for step in range(s0, s1):
+                k = step % NK
+                if step < NK:
+                    lhsT, ls = vfp[k][g][:, 2 * t * P:2 * (t + 1) * P].bitcast(FP4X4), vfs[g][:, k, cols]
+                    key = ("f", k, h)
+                else:
+                    lhsT, ls = vnc[g][k][:, cols].bitcast(FP8X4), vns[g][k][:, cols]
+                    key = ("n", k, h)
+                nc.tensor.matmul_mx(
+                    out=acc[g, h, t][:], lhsT=lhsT, lhsT_scale=ls, rhs=codes[key][:].bitcast(FP8X4),
+                    rhs_scale=scales[key][:], start=(step == 0), stop=(step == 2 * NK - 1))
+
+        def vt(g, h, c, b):
+            x = bank(b, [P, 2, 256], F32)
+            vts[g, h, c] = x
+            for i in range(2):
+                words = vel[g][h][:, 2 * c + i, :].bitcast(F32)
+                for u in range(2):
+                    nc.tensor.transpose(x[:, u, i * P:(i + 1) * P], words[:, u:256:2], ident[:])
+
+        def dr(g, h, t, e):
+            if (g, h) not in cscs:
+                cscs[g, h] = work.tile([P, T, W], F32, name="csc", tag="csc", bufs=2)
+            dst, src, by = cscs[g, h][:, t, :], acc[g, h, t][:], rbeta[:, g, t:t + 1]
+            if e == "S":
+                nc.scalar.activation(out=dst, in_=src, func=COPY, scale=by)
             else:
-                lhsT = vnc[g][k][:, cols].bitcast(FP8X4)
-                ls = vns[g][k][:, cols]
-                rhs, rs = hnc[k][h], hns[k][h]
-            nc.tensor.matmul_mx(
-                out=cb[t][:], lhsT=lhsT, lhsT_scale=ls, rhs=rhs[:].bitcast(FP8X4), rhs_scale=rs[:],
-                start=(step == 0), stop=(step == 2 * NK - 1),
-            )
+                nc.vector.tensor_scalar(out=dst, in0=src, scalar1=by, scalar2=None, op0=MULT)
 
-        def vel_t(g, h):
-            res = []
-            for c in range(2):
-                x = psum.tile([P, 2, 256], F32, name="vt", tag="vt", bufs=2)
-                for b in range(2):
-                    words = vel[g][h][:, 2 * c + b, :].bitcast(F32)
-                    for u in range(2):
-                        nc.tensor.transpose(x[:, u, b * P:(b + 1) * P], words[:, u:256:2], ident[:])
-                res.append(x)
-            return res
-
-        def drain(cb, g):
-            x = work.tile([P, T, W], F32, name="csc", tag="csc", bufs=2)
-            for t in range(T):
-                nc.scalar.activation(out=x[:, t, :], in_=cb[t][:], func=COPY, scale=rbeta[:, g, t:t + 1])
-            return x
-
-        def d_add(x, vt, c, dst):
+        def da(g, h, c):
+            if (g, h) not in dbfs:
+                dbfs[g, h] = work.tile([P, W * T], BF16, name="dbf", tag="dbf", bufs=2, align_bytes=64)
             nc.vector.tensor_tensor(
-                out=dst[:, 1024 * c:1024 * (c + 1)].rearrange("p (r u e) -> p r u e", u=2, e=2),
-                in0=x[:, :, 256 * c:256 * (c + 1)].rearrange("p (u e) r -> p r u e", e=2),
-                in1=vt[c][:].bitcast(BF16).rearrange("p u (r e) -> p r u e", e=2),
+                out=dbfs[g, h][:, 1024 * c:1024 * (c + 1)].rearrange("p (r u e) -> p r u e", u=2, e=2),
+                in0=cscs[g, h][:, :, 256 * c:256 * (c + 1)].rearrange("p (u e) r -> p r u e", e=2),
+                in1=vts[g, h, c][:].bitcast(BF16).rearrange("p u (r e) -> p r u e", e=2),
                 op=ADD,
             )
 
-        def d_quant(g, h, dst, lo, hi):
+        def dq(g, h, c):
+            s = part(c)
             nc.vector.quantize_mx(
-                out=dc[g][h][:, lo:hi].bitcast(FP8X4), scales=ds[g][h][:, lo:hi], in_=dst[:, T * lo:T * hi])
+                out=dc[g][h][:, s].bitcast(FP8X4), scales=ds[g][h][:, s], in_=dbfs[g, h][:, T * s.start:T * s.stop])
 
-        def d_tile():
-            return work.tile([P, W * T], BF16, name="dbf", tag="dbf", bufs=2, align_bytes=64)
-
-        def out_mm(bank, h, a, g):
+        def om(h, a, g0, g1, b=None):
+            if g0 == 0:
+                obs[h, a] = bank(b, [P, L], F32)
             cols = slice(a * P, (a + 1) * P)
-            nc.tensor.matmul_mx(
-                out=bank[:], lhsT=dc[g][h][:, cols].bitcast(FP8X4), lhsT_scale=ds[g][h][:, cols],
-                rhs=prw[:, g, :].bitcast(FP4X4), rhs_scale=prs[:, g, :], start=(g == 0), stop=(g == NG - 1))
+            for g in range(g0, g1):
+                nc.tensor.matmul_mx(
+                    out=obs[h, a][:], lhsT=dc[g][h][:, cols].bitcast(FP8X4), lhsT_scale=ds[g][h][:, cols],
+                    rhs=prw[:, g, :].bitcast(FP4X4), rhs_scale=prs[:, g, :], start=(g == 0), stop=(g == NG - 1))
 
-        def out_bank():
-            return psum.tile([P, L], F32, name="ob", tag="ob", bufs=2)
-
-        def store(bank, h, a, engine):
+        def st(h, a, e):
             x = work.tile([P, L], F32, name="res", tag="res", bufs=4)
-            if engine == "s":
-                nc.scalar.copy(out=x[:], in_=bank[:])
-            else:
-                nc.vector.tensor_copy(out=x[:], in_=bank[:])
+            copy_on(e, x[:], obs[h, a][:])
             r = (h * T + a) * P
             nc.sync.dma_start(out=out[r:r + P, :], in_=x[:])
 
-        hf_ilv("v", 0, 0)
-        perm_words(0, 0)
-        perm_scales(0)
-        q_hf(0, 0)
-        c1 = banks()
-        for t in range(T):
-            mm(c1, 0, 0, t, 0)
-        widen(0, 0)
-        perm_words(1, 0)
-        hf_ilv("v", 1, 0)
-        hn_ilv("s", 0, 0, 256, W)
-        ilv_v("v", 0, 0)
-        q_hf(1, 0)
-        for t in range(T):
-            mm(c1, 0, 0, t, 1)
-        widen(1, 0)
-        hn_ilv("v", 0, 0, 0, 256)
-        q_v(0, 0)
-        ilv_v("v", 0, 1, 0, 2)
-        q_hn(0, 0)
-        vt1 = vel_t(0, 0)
-        for t in range(T):
-            mm(c1, 0, 0, t, 2)
-        ilv_v("s", 0, 1, 2, T)
-        hn_ilv("v", 1, 0)
-        nc.vector.reciprocal(out=rbeta[:].rearrange("p g t -> p (g t)"), in_=beta_sb[:].rearrange("p g t -> p (g t)"))
-        q_v(0, 1)
-        q_hn(1, 0)
-        for t in range(T):
-            mm(c1, 0, 0, t, 3)
-
-        perm_words(0, 1)
-        ilv_v("s", 1, 0, 2, T)
-        ilv_v("v", 1, 0, 0, 2)
-        perm_words(1, 1)
-        perm_scales(1)
-        q_v(1, 0)
-        ilv_v("v", 1, 1)
-        perm_words(0, 2)
-        q_v(1, 1)
-
-        x1 = drain(c1, 0)
-
-        def unit(g, h, extra=()):
-            cb = banks()
-            vt = None
-            for t in range(T):
-                for step in range(2 * NK):
-                    mm(cb, g, h, t, step)
-                if t == 2:
-                    vt = vel_t(g, h)
-            return cb, vt
-
-        def d_step(x, vt, g, h):
-            dst = d_tile()
-            d_add(x, vt, 0, dst)
-            d_add(x, vt, 1, dst)
-            return dst
-
-        d1 = d_step(x1, vt1, 0, 0)
-        c2, vt2 = unit(1, 0)
-        hf_ilv("g", 0, 1)
-        ilv_v("s", 2, 1)
-        ilv_v("v", 2, 0)
-        d_quant(0, 0, d1, 0, W)
-        perm_words(1, 2)
-        perm_scales(2)
-        q_v(2, 0)
-        widen(0, 1)
-        q_v(2, 1)
-
-        x2 = drain(c2, 1)
-        hf_ilv("v", 1, 1)
-        q_hf(0, 1)
-        d2 = d_step(x2, vt2, 1, 0)
-        c3, vt3 = unit(2, 0)
-        widen(1, 1)
-        q_hf(1, 1)
-        hn_ilv("v", 0, 1)
-        d_quant(1, 0, d2, 0, W)
-        hn_ilv("s", 1, 1, 256, W)
-        hn_ilv("v", 1, 1, 0, 256)
-        q_hn(0, 1)
-
-        x3 = drain(c3, 2)
-        q_hn(1, 1)
-        d3 = d_step(x3, vt3, 2, 0)
-        d_quant(2, 0, d3, 0, W)
-        c4, vt4 = unit(0, 1)
-
-        x4 = drain(c4, 0)
-        d4 = d_step(x4, vt4, 0, 1)
-        d_quant(0, 1, d4, 0, W)
-        for a in range(2):
-            ob = out_bank()
-            for g in range(NG):
-                out_mm(ob, 0, a, g)
-            store(ob, 0, a, "s" if a else "v")
-        c5, vt5 = unit(1, 1)
-
-        x5 = drain(c5, 1)
-        d5 = d_step(x5, vt5, 1, 1)
-        d_quant(1, 1, d5, 0, W)
-        c6, vt6 = unit(2, 1)
-
-        obs = []
-        for a in range(2, T):
-            ob = out_bank()
-            for g in range(NG):
-                out_mm(ob, 0, a, g)
-            obs.append(ob)
-        x6 = drain(c6, 2)
-        store(obs[0], 0, 2, "v")
-        store(obs[1], 0, 3, "s")
-        last = [psum.tile([P, L], F32, name="c%d" % a, tag="c%d" % a) for a in range(T)]
-        for a in range(T):
-            for g in range(2):
-                out_mm(last[a], 1, a, g)
-        d6 = d_tile()
-        d_add(x6, vt6, 0, d6)
-        d_quant(2, 1, d6, 0, 256)
-        d_add(x6, vt6, 1, d6)
-        d_quant(2, 1, d6, 256, W)
-        for a in range(T):
-            out_mm(last[a], 1, a, 2)
-        for a in range(T):
-            store(last[a], 1, a, "s" if a % 2 == 0 else "v")
+        ld("hn", 0)
+        ld("hn", 1)
+        wid(0, 0, 2, "V")
+        wid(1, 0, 2, "V")
+        ld("vfw", 1)
+        pw(1, 2)
+        ld("hf", 1, 0)
+        wid(0, 1, 2, "S")
+        ld("hf", 0, 0)
+        ilv(("n", 0, 0), 0, "S")
+        ld("vfw", 0)
+        ilv(("n", 1, 0), 1, "S")
+        ilv(("n", 1, 0), 0, "V")
+        ilv(("n", 0, 0), 1, "S")
+        ilv(("f", 0, 0), 0, "S")
+        pw(1, 1)
+        ld("vfs")
+        ld("vn", 2, 0)
+        ilv(("f", 1, 0), 0, "V")
+        pw(1, 0)
+        ilv(("f", 1, 0), 1, "S")
+        pw(0, 2)
+        ilv(("f", 0, 0), 1, "V")
+        ps(2)
+        q(("f", 0, 0), 2)
+        ld("vn", 2, 1)
+        pw(0, 0)
+        ld("vn", 0, 0)
+        q(("f", 1, 0), 0)
+        q(("f", 1, 0), 1)
+        ilv(("v", 2, 0), 1, "S")
+        mm(2, 0, 1, 0, 2, 0)
+        ps(0)
+        ld("vn", 0, 1)
+        q(("n", 1, 0), 2)
+        ld("vn", 1, 0)
+        mm(2, 0, 3, 0, 1, 7)
+        ilv(("v", 2, 1), 0, "S")
+        q(("n", 0, 0), 2)
+        rb()
+        ld("hf", 0, 1)
+        mm(2, 0, 2, 0, 2, 2)
+        mm(0, 0, 2, 0, 2, 3)
+        ld("vn", 1, 1)
+        ilv(("v", 2, 0), 0, "S")
+        ld("vel", 2, 0)
+        ld("prw")
+        ilv(("v", 0, 0), 0, "S")
+        mm(0, 0, 1, 0, 2, 5)
+        mm(2, 0, 3, 1, 2)
+        ilv(("v", 2, 1), 1, "V")
+        q(("v", 2, 0), 2)
+        ld("vel", 0, 0)
+        q(("v", 2, 1), 2)
+        ilv(("v", 0, 1), 1, "S")
+        mm(0, 0, 3, 0, 2, 4)
+        mm(2, 0, 0, 0, 4, 6)
+        mm(2, 0, 2, 2, 4)
+        ilv(("v", 0, 0), 1, "S")
+        ilv(("v", 0, 1), 0, "V")
+        pw(0, 1)
+        dr(2, 0, 2, "S")
+        q(("v", 0, 1), 0)
+        q(("v", 0, 0), 0)
+        mm(2, 0, 3, 2, 4)
+        ps(1)
+        q(("v", 0, 0), 1)
+        ilv(("v", 1, 1), 0, "V")
+        q(("v", 0, 1), 1)
+        mm(2, 0, 1, 2, 4)
+        ilv(("v", 1, 0), 0, "V")
+        mm(0, 0, 1, 2, 4)
+        mm(0, 0, 0, 0, 4, 2)
+        mm(0, 0, 2, 2, 4)
+        dr(2, 0, 3, "S")
+        q(("v", 1, 1), 0)
+        dr(2, 0, 1, "S")
+        ilv(("n", 0, 1), 0, "V")
+        mm(0, 0, 3, 2, 4)
+        dr(0, 0, 1, "S")
+        ilv(("f", 0, 1), 0, "V")
+        q(("v", 1, 0), 0)
+        ilv(("v", 1, 0), 1, "S")
+        dr(2, 0, 0, "S")
+        ld("vel", 0, 1)
+        ld("hf", 1, 1)
+        ilv(("v", 1, 1), 1, "S")
+        q(("v", 1, 0), 1)
+        vt(2, 0, 0, 5)
+        vt(2, 0, 1, 0)
+        mm(1, 0, 1, 0, 4, 1)
+        mm(1, 0, 0, 0, 4, 6)
+        da(2, 0, 0)
+        dr(0, 0, 2, "S")
+        ilv(("f", 0, 1), 1, "S")
+        q(("v", 1, 1), 1)
+        ilv(("f", 1, 1), 1, "S")
+        da(2, 0, 1)
+        q(("f", 0, 1), 2)
+        mm(1, 0, 2, 0, 4, 7)
+        ld("vel", 1, 0)
+        mm(1, 0, 3, 0, 4, 3)
+        dr(1, 0, 1, "S")
+        ilv(("n", 0, 1), 1, "V")
+        dr(1, 0, 3, "S")
+        vt(0, 0, 0, 0)
+        vt(0, 0, 1, 5)
+        ld("prs")
+        ld("vel", 2, 1)
+        ilv(("f", 1, 1), 0, "V")
+        dr(0, 0, 0, "S")
+        dr(1, 0, 2, "S")
+        q(("n", 0, 1), 2)
+        wid(1, 1, 1, "S")
+        dr(0, 0, 3, "S")
+        q(("f", 1, 1), 2)
+        wid(1, 1, 0, "V")
+        vt(1, 0, 0, 1)
+        vt(1, 0, 1, 3)
+        dr(1, 0, 0, "V")
+        ilv(("n", 1, 1), 0, "V")
+        da(1, 0, 1)
+        ilv(("n", 1, 1), 1, "S")
+        q(("n", 1, 1), 0)
+        q(("n", 1, 1), 1)
+        da(1, 0, 0)
+        ld("vel", 1, 1)
+        mm(0, 1, 1, 0, 3, 2)
+        mm(2, 1, 0, 0, 3, 7)
+        mm(0, 1, 0, 0, 3, 6)
+        dq(2, 0, 2)
+        mm(2, 1, 3, 0, 3, 4)
+        mm(0, 1, 2, 0, 4, 3)
+        mm(2, 1, 3, 3, 4)
+        mm(0, 1, 0, 3, 4)
+        mm(0, 1, 1, 3, 4)
+        da(0, 0, 0)
+        mm(2, 1, 0, 3, 4)
+        da(0, 0, 1)
+        dr(2, 1, 0, "V")
+        mm(0, 1, 3, 0, 4, 1)
+        dr(0, 1, 2, "S")
+        dr(0, 1, 3, "S")
+        mm(2, 1, 1, 0, 4, 3)
+        dr(0, 1, 1, "S")
+        dr(0, 1, 0, "S")
+        vt(0, 1, 1, 1)
+        vt(2, 1, 0, 5)
+        dq(1, 0, 2)
+        vt(1, 1, 0, 6)
+        da(0, 1, 1)
+        dr(2, 1, 1, "S")
+        dr(2, 1, 3, "S")
+        vt(0, 1, 0, 0)
+        dq(0, 0, 2)
+        vt(2, 1, 1, 3)
+        da(0, 1, 0)
+        mm(2, 1, 2, 0, 4, 2)
+        mm(1, 1, 3, 0, 4, 1)
+        dr(2, 1, 2, "S")
+        mm(1, 1, 1, 0, 4, 7)
+        da(2, 1, 0)
+        da(2, 1, 1)
+        mm(1, 1, 0, 0, 4, 4)
+        dq(0, 1, 2)
+        dr(1, 1, 0, "S")
+        om(0, 2, 0, 3, 0)
+        mm(1, 1, 2, 0, 4, 2)
+        om(0, 1, 0, 3, 3)
+        dr(1, 1, 3, "V")
+        st(0, 2, "S")
+        dq(2, 1, 2)
+        om(0, 0, 0, 3, 4)
+        dr(1, 1, 1, "V")
+        om(0, 3, 0, 3, 1)
+        dr(1, 1, 2, "V")
+        st(0, 1, "S")
+        da(1, 1, 0)
+        dq(1, 1, 0)
+        st(0, 0, "S")
+        vt(1, 1, 1, 3)
+        om(1, 0, 0, 3, 4)
+        st(0, 3, "S")
+        da(1, 1, 1)
+        dq(1, 1, 1)
+        om(1, 3, 0, 1, 2)
+        om(1, 1, 0, 3, 0)
+        om(1, 2, 0, 3, 6)
+        om(1, 3, 1, 3)
+        st(1, 0, "S")
+        st(1, 1, "S")
+        st(1, 2, "V")
+        st(1, 3, "V")

@@ -165,14 +165,14 @@ def tile_eqprop_projected_update_s3_kernel(
 
         def pw(k, g):
             nc.vector.tensor_copy(
-                out=vfp[k][g][:].rearrange("p (t m b) -> p t m b", t=T, b=2),
-                in_=vfr[k][:, 2 * KP * g:2 * KP * (g + 1)].rearrange("p (m t b) -> p t m b", t=T, b=2),
+                out=vfp[k][g][:].rearrange("p (t m b) -> p m t b", t=T, b=2),
+                in_=vfr[k][:, 2 * KP * g:2 * KP * (g + 1)].rearrange("p (m t b) -> p m t b", t=T, b=2),
             )
 
         def ps(g):
             nc.vector.tensor_copy(
-                out=vfs[g][:].rearrange("p k (t m) -> p k t m", t=T),
-                in_=vfs_raw[:, :, KP * g:KP * (g + 1)].rearrange("p k (m t) -> p k t m", t=T),
+                out=vfs[g][:].rearrange("p k (t m) -> p k m t", t=T),
+                in_=vfs_raw[:, :, KP * g:KP * (g + 1)].rearrange("p k (m t) -> p k m t", t=T),
             )
 
         def rb():
@@ -200,12 +200,12 @@ def tile_eqprop_projected_update_s3_kernel(
                     rhs_scale=scales[key][:], start=(step == 0), stop=(step == 2 * NK - 1))
 
         def vt(g, h, c, b):
-            x = bank(b, [P, 2, 256], F32)
+            x = bank(b, [P, 256, 2], F32)
             vts[g, h, c] = x
             for i in range(2):
                 words = vel[g][h][:, 2 * c + i, :].bitcast(F32)
                 for u in range(2):
-                    nc.tensor.transpose(x[:, u, i * P:(i + 1) * P], words[:, u:256:2], ident[:])
+                    nc.tensor.transpose(x[:, i * P:(i + 1) * P, u], words[:, u:256:2], ident[:])
 
         def dr(g, h, t, e):
             if (g, h) not in cscs:
@@ -220,9 +220,9 @@ def tile_eqprop_projected_update_s3_kernel(
             if (g, h) not in dbfs:
                 dbfs[g, h] = work.tile([P, W * T], BF16, name="dbf", tag="dbf", bufs=2, align_bytes=64)
             nc.vector.tensor_tensor(
-                out=dbfs[g, h][:, 1024 * c:1024 * (c + 1)].rearrange("p (r u e) -> p r u e", u=2, e=2),
-                in0=cscs[g, h][:, :, 256 * c:256 * (c + 1)].rearrange("p (u e) r -> p r u e", e=2),
-                in1=vts[g, h, c][:].bitcast(BF16).rearrange("p u (r e) -> p r u e", e=2),
+                out=dbfs[g, h][:, 1024 * c:1024 * (c + 1)].rearrange("p (x i t) -> p x t i", i=4, t=T),
+                in0=cscs[g, h][:, :, 256 * c:256 * (c + 1)].rearrange("p t (x i) -> p x t i", i=4),
+                in1=vts[g, h, c][:].bitcast(BF16).rearrange("p r t -> p (r t)").rearrange("p (x i t) -> p x t i", i=4, t=T),
                 op=ADD,
             )
 

@@ -246,196 +246,198 @@ def tile_eqprop_projected_update_s3_kernel(
             r = (h * T + a) * P
             nc.sync.dma_start(out=out[r:r + P, :], in_=x[:])
 
-        ld("hn", 0)
         ld("hn", 1)
-        wid(0, 0, 2, "V")
-        wid(1, 0, 2, "V")
-        ld("vfw", 1)
-        pw(1, 2)
-        ld("hf", 1, 0)
-        wid(0, 1, 2, "S")
+        ld("hn", 0)
         ld("hf", 0, 0)
-        ilv(("n", 0, 0), 0, "S")
-        ld("vfw", 0)
-        ilv(("n", 1, 0), 1, "S")
-        ilv(("n", 1, 0), 0, "V")
-        ilv(("n", 0, 0), 1, "S")
-        ilv(("f", 0, 0), 0, "S")
-        pw(1, 1)
         ld("vfs")
-        ld("vn", 2, 0)
-        ilv(("f", 1, 0), 0, "V")
-        pw(1, 0)
-        ilv(("f", 1, 0), 1, "S")
-        pw(0, 2)
-        ilv(("f", 0, 0), 1, "V")
-        ps(2)
-        q(("f", 0, 0), 2)
-        ld("vn", 2, 1)
-        pw(0, 0)
+        ld("hf", 1, 0)
+        ld("vfw", 0)
+        ld("vfw", 1)
         ld("vn", 0, 0)
-        q(("f", 1, 0), 0)
-        q(("f", 1, 0), 1)
-        ilv(("v", 2, 0), 1, "S")
-        mm(2, 0, 1, 0, 2, 0)
-        ps(0)
         ld("vn", 0, 1)
-        q(("n", 1, 0), 2)
-        ld("vn", 1, 0)
-        mm(2, 0, 3, 0, 1, 7)
-        ilv(("v", 2, 1), 0, "S")
-        q(("n", 0, 0), 2)
-        rb()
-        ld("hf", 0, 1)
-        mm(2, 0, 2, 0, 2, 2)
-        mm(0, 0, 2, 0, 2, 3)
-        ld("vn", 1, 1)
-        ilv(("v", 2, 0), 0, "S")
-        ld("vel", 2, 0)
-        ld("prw")
-        ilv(("v", 0, 0), 0, "S")
-        mm(0, 0, 1, 0, 2, 5)
-        mm(2, 0, 3, 1, 2)
-        ilv(("v", 2, 1), 1, "V")
-        q(("v", 2, 0), 2)
         ld("vel", 0, 0)
-        q(("v", 2, 1), 2)
-        ilv(("v", 0, 1), 1, "S")
-        mm(0, 0, 3, 0, 2, 4)
-        mm(2, 0, 0, 0, 4, 6)
-        mm(2, 0, 2, 2, 4)
-        ilv(("v", 0, 0), 1, "S")
-        ilv(("v", 0, 1), 0, "V")
-        pw(0, 1)
-        dr(2, 0, 2, "S")
-        q(("v", 0, 1), 0)
-        q(("v", 0, 0), 0)
-        mm(2, 0, 3, 2, 4)
-        ps(1)
-        q(("v", 0, 0), 1)
-        ilv(("v", 1, 1), 0, "V")
-        q(("v", 0, 1), 1)
-        mm(2, 0, 1, 2, 4)
-        ilv(("v", 1, 0), 0, "V")
-        mm(0, 0, 1, 2, 4)
-        mm(0, 0, 0, 0, 4, 2)
-        mm(0, 0, 2, 2, 4)
-        dr(2, 0, 3, "S")
-        q(("v", 1, 1), 0)
-        dr(2, 0, 1, "S")
-        ilv(("n", 0, 1), 0, "V")
-        mm(0, 0, 3, 2, 4)
-        dr(0, 0, 1, "S")
-        ilv(("f", 0, 1), 0, "V")
-        q(("v", 1, 0), 0)
-        ilv(("v", 1, 0), 1, "S")
-        dr(2, 0, 0, "S")
-        ld("vel", 0, 1)
+        ld("hf", 0, 1)
         ld("hf", 1, 1)
-        ilv(("v", 1, 1), 1, "S")
-        q(("v", 1, 0), 1)
-        vt(2, 0, 0, 5)
-        vt(2, 0, 1, 0)
-        mm(1, 0, 1, 0, 4, 1)
-        mm(1, 0, 0, 0, 4, 6)
-        da(2, 0, 0)
-        dr(0, 0, 2, "S")
-        ilv(("f", 0, 1), 1, "S")
-        q(("v", 1, 1), 1)
-        ilv(("f", 1, 1), 1, "S")
-        da(2, 0, 1)
-        q(("f", 0, 1), 2)
-        mm(1, 0, 2, 0, 4, 7)
+        ld("vel", 0, 1)
+        ld("vn", 1, 1)
+        ld("vn", 1, 0)
+        ld("vel", 2, 0)
+        ld("vn", 2, 1)
+        ld("vn", 2, 0)
         ld("vel", 1, 0)
-        mm(1, 0, 3, 0, 4, 3)
-        dr(1, 0, 1, "S")
-        ilv(("n", 0, 1), 1, "V")
-        dr(1, 0, 3, "S")
-        vt(0, 0, 0, 0)
-        vt(0, 0, 1, 5)
+        ld("vel", 1, 1)
         ld("prs")
         ld("vel", 2, 1)
+        ld("prw")
+        rb()
+        wid(1, 1, 2, "V")
+        wid(0, 1, 2, "V")
+        wid(0, 0, 2, "V")
+        wid(1, 0, 2, "S")
+        ilv(("n", 1, 0), 1, "S")
+        ilv(("f", 0, 0), 0, "S")
+        ilv(("f", 0, 0), 1, "S")
+        ilv(("n", 1, 0), 0, "V")
+        ilv(("n", 0, 0), 0, "V")
+        ilv(("n", 0, 0), 1, "V")
+        ilv(("f", 1, 0), 0, "S")
+        ilv(("f", 1, 0), 1, "S")
+        ilv(("v", 0, 0), 1, "S")
+        ilv(("v", 0, 1), 0, "S")
+        ilv(("v", 0, 1), 1, "S")
+        ilv(("f", 0, 1), 0, "S")
+        ps(0)
+        q(("f", 0, 0), 2)
+        pw(0, 0)
+        pw(1, 0)
+        mm(0, 0, 3, 0, 1, 2)
+        mm(0, 0, 1, 0, 1, 7)
+        q(("n", 0, 0), 2)
+        q(("f", 1, 0), 2)
+        ilv(("v", 0, 0), 0, "V")
+        q(("n", 1, 0), 2)
+        q(("v", 0, 0), 2)
+        q(("v", 0, 1), 0)
+        mm(0, 0, 0, 0, 2, 5)
+        mm(0, 0, 2, 0, 2, 0)
+        ilv(("n", 0, 1), 1, "V")
+        vt(0, 0, 1, 1)
+        vt(0, 0, 0, 3)
+        q(("v", 0, 1), 1)
+        ilv(("f", 0, 1), 1, "V")
+        ilv(("n", 0, 1), 0, "V")
         ilv(("f", 1, 1), 0, "V")
-        dr(0, 0, 0, "S")
-        dr(1, 0, 2, "S")
-        q(("n", 0, 1), 2)
-        wid(1, 1, 1, "S")
-        dr(0, 0, 3, "S")
+        mm(0, 0, 1, 1, 4)
+        mm(0, 0, 3, 1, 4)
+        mm(0, 0, 2, 2, 4)
+        mm(0, 0, 0, 2, 4)
+        ilv(("f", 1, 1), 1, "S")
+        q(("f", 0, 1), 2)
         q(("f", 1, 1), 2)
-        wid(1, 1, 0, "V")
-        vt(1, 0, 0, 1)
-        vt(1, 0, 1, 3)
-        dr(1, 0, 0, "V")
+        q(("n", 0, 1), 2)
+        dr(0, 0, 1, "S")
+        dr(0, 0, 2, "S")
+        dr(0, 0, 0, "S")
+        vt(0, 1, 0, 6)
+        vt(0, 1, 1, 4)
+        mm(0, 1, 0, 0, 1, 7)
+        mm(0, 1, 3, 0, 2, 0)
+        mm(0, 1, 1, 0, 3, 5)
+        mm(0, 1, 3, 2, 3)
+        mm(0, 1, 0, 1, 3)
         ilv(("n", 1, 1), 0, "V")
-        da(1, 0, 1)
+        pw(0, 1)
         ilv(("n", 1, 1), 1, "S")
-        q(("n", 1, 1), 0)
-        q(("n", 1, 1), 1)
-        da(1, 0, 0)
-        ld("vel", 1, 1)
-        mm(0, 1, 1, 0, 3, 2)
-        mm(2, 1, 0, 0, 3, 7)
-        mm(0, 1, 0, 0, 3, 6)
-        dq(2, 0, 2)
-        mm(2, 1, 3, 0, 3, 4)
-        mm(0, 1, 2, 0, 4, 3)
-        mm(2, 1, 3, 3, 4)
-        mm(0, 1, 0, 3, 4)
+        q(("n", 1, 1), 2)
+        dr(0, 0, 3, "S")
+        ps(1)
+        mm(0, 1, 2, 0, 2, 2)
         mm(0, 1, 1, 3, 4)
-        da(0, 0, 0)
-        mm(2, 1, 0, 3, 4)
-        da(0, 0, 1)
-        dr(2, 1, 0, "V")
-        mm(0, 1, 3, 0, 4, 1)
-        dr(0, 1, 2, "S")
-        dr(0, 1, 3, "S")
-        mm(2, 1, 1, 0, 4, 3)
+        mm(0, 1, 3, 3, 4)
+        mm(0, 1, 0, 3, 4)
+        mm(0, 1, 2, 2, 4)
+        ilv(("v", 1, 0), 0, "S")
         dr(0, 1, 1, "S")
+        dr(0, 1, 3, "S")
+        dr(0, 1, 2, "S")
         dr(0, 1, 0, "S")
-        vt(0, 1, 1, 1)
-        vt(2, 1, 0, 5)
-        dq(1, 0, 2)
-        vt(1, 1, 0, 6)
-        da(0, 1, 1)
-        dr(2, 1, 1, "S")
-        dr(2, 1, 3, "S")
-        vt(0, 1, 0, 0)
-        dq(0, 0, 2)
-        vt(2, 1, 1, 3)
+        pw(1, 1)
+        ilv(("v", 1, 1), 0, "V")
+        q(("v", 1, 0), 0)
+        q(("v", 1, 1), 0)
+        mm(1, 1, 1, 0, 2, 5)
+        mm(1, 0, 1, 0, 2, 0)
+        mm(1, 0, 0, 0, 4, 2)
+        mm(1, 1, 1, 2, 4)
+        mm(1, 1, 0, 0, 4, 7)
+        mm(1, 0, 1, 2, 4)
+        da(0, 0, 1)
+        da(0, 0, 0)
+        ilv(("v", 1, 1), 1, "S")
+        ilv(("v", 1, 0), 1, "S")
+        q(("v", 1, 1), 1)
+        q(("v", 1, 0), 1)
+        mm(1, 1, 2, 0, 1, 1)
+        mm(1, 0, 2, 0, 4, 3)
         da(0, 1, 0)
-        mm(2, 1, 2, 0, 4, 2)
-        mm(1, 1, 3, 0, 4, 1)
-        dr(2, 1, 2, "S")
-        mm(1, 1, 1, 0, 4, 7)
-        da(2, 1, 0)
-        da(2, 1, 1)
-        mm(1, 1, 0, 0, 4, 4)
-        dq(0, 1, 2)
+        dr(1, 1, 1, "S")
         dr(1, 1, 0, "S")
-        om(0, 2, 0, 3, 0)
-        mm(1, 1, 2, 0, 4, 2)
-        om(0, 1, 0, 3, 3)
-        dr(1, 1, 3, "V")
-        st(0, 2, "S")
-        dq(2, 1, 2)
-        om(0, 0, 0, 3, 4)
-        dr(1, 1, 1, "V")
-        om(0, 3, 0, 3, 1)
-        dr(1, 1, 2, "V")
-        st(0, 1, "S")
+        ps(2)
+        mm(1, 0, 3, 0, 4, 7)
+        mm(1, 1, 2, 1, 4)
+        mm(1, 1, 3, 0, 4, 5)
+        ilv(("v", 2, 0), 0, "S")
+        ilv(("v", 2, 1), 0, "S")
+        vt(1, 0, 0, 6)
+        da(0, 1, 1)
+        dr(1, 1, 2, "S")
+        dr(1, 0, 1, "S")
+        dr(1, 0, 0, "S")
+        dr(1, 1, 3, "S")
+        q(("v", 2, 0), 0)
+        vt(1, 0, 1, 1)
+        vt(1, 1, 1, 0)
+        vt(1, 1, 0, 2)
+        pw(0, 2)
+        dq(0, 0, 2)
+        pw(1, 2)
+        mm(2, 0, 1, 0, 1, 4)
+        q(("v", 2, 1), 0)
+        mm(2, 1, 0, 0, 4, 5)
+        mm(2, 0, 1, 1, 4)
         da(1, 1, 0)
-        dq(1, 1, 0)
-        st(0, 0, "S")
-        vt(1, 1, 1, 3)
-        om(1, 0, 0, 3, 4)
-        st(0, 3, "S")
+        ilv(("v", 2, 0), 1, "S")
+        ilv(("v", 2, 1), 1, "S")
+        dr(1, 0, 2, "S")
+        dr(1, 0, 3, "S")
+        mm(2, 1, 1, 0, 4, 2)
+        q(("v", 2, 1), 1)
+        q(("v", 2, 0), 1)
         da(1, 1, 1)
-        dq(1, 1, 1)
-        om(1, 3, 0, 1, 2)
-        om(1, 1, 0, 3, 0)
-        om(1, 2, 0, 3, 6)
-        om(1, 3, 1, 3)
+        dq(0, 1, 2)
+        mm(2, 1, 3, 0, 4, 3)
+        mm(2, 0, 2, 0, 4, 0)
+        mm(2, 1, 2, 0, 4, 7)
+        dr(2, 1, 3, "S")
+        dr(2, 1, 1, "S")
+        dr(2, 1, 2, "S")
+        dr(2, 1, 0, "S")
+        da(1, 0, 0)
+        da(1, 0, 1)
+        vt(2, 1, 0, 2)
+        vt(2, 1, 1, 3)
+        vt(2, 0, 0, 7)
+        dq(1, 1, 2)
+        dq(1, 0, 2)
+        dr(2, 0, 1, "S")
+        mm(2, 0, 0, 0, 4, 6)
+        mm(2, 0, 3, 0, 4, 5)
+        dr(2, 0, 0, "S")
+        dr(2, 0, 3, "S")
+        dr(2, 0, 2, "S")
+        da(2, 1, 0)
+        dq(2, 1, 0)
+        om(1, 1, 0, 2, 6)
+        om(1, 0, 0, 3, 4)
+        om(1, 1, 2, 3)
+        da(2, 1, 1)
+        dq(2, 1, 1)
+        om(1, 2, 0, 3, 2)
+        da(2, 0, 0)
         st(1, 0, "S")
         st(1, 1, "S")
-        st(1, 2, "V")
-        st(1, 3, "V")
+        st(1, 2, "S")
+        dq(2, 0, 0)
+        om(1, 3, 0, 3, 4)
+        vt(2, 0, 1, 3)
+        om(0, 0, 0, 3, 1)
+        om(0, 1, 0, 3, 6)
+        da(2, 0, 1)
+        dq(2, 0, 1)
+        om(0, 2, 0, 3, 3)
+        st(1, 3, "S")
+        st(0, 0, "S")
+        st(0, 1, "V")
+        st(0, 2, "S")
+        om(0, 3, 0, 3, 1)
+        st(0, 3, "V")

from contextlib import ExitStack

import concourse.mybir as mybir
from concourse.masks import make_identity

B, I, J, L = 1024, 1024, 1536, 512
FLOPS = 2 * 2 * B * I * J + 2 * I * J * L

F32 = mybir.dt.float32
BF16 = mybir.dt.bfloat16
I32 = mybir.dt.int32
U32 = mybir.dt.uint32
U8 = mybir.dt.uint8
FP8 = mybir.dt.float8_e4m3fn
FP8X4 = mybir.dt.float8_e4m3fn_x4
FP4X4 = mybir.dt.float4_e2m1fn_x4
COPY = mybir.ActivationFunctionType.Copy
MULT = mybir.AluOpType.mult
ADD = mybir.AluOpType.add

P = 128
T = 4
KP = P * T
W = 512
NG = J // KP
NH = I // W
NK = B // KP


def tile_eqprop_projected_update_s3_kernel(
    tc, h_nudged_bytes, h_nudged_scale, v_nudged, h_free_neg, v_free_words, v_free_scales,
    beta, velocity, proj_words, proj_scales, out,
):
    nc = tc.nc
    with ExitStack() as ctx:
        keep = ctx.enter_context(tc.tile_pool(name="keep", bufs=1))
        work = ctx.enter_context(tc.tile_pool(name="work", bufs=2))
        psum = ctx.enter_context(tc.psum_pool(name="psum", bufs=1))

        def kept(name, shape, dtype):
            return keep.tile(shape, dtype, name=name, tag=name, align_bytes=64)

        ident = kept("ident", [P, P], F32)
        make_identity(nc, ident[:])
        vfs_raw = kept("vfs_raw", [P, NK, J], U8)
        prs = kept("prs", [P, NG, L], U8)
        warm = kept("warm", [P, 1], F32)

        hsc = kept("hsc", [P, NK, T], F32)
        beta_sb = kept("beta_sb", [P, NG, T], BF16)
        rbeta = kept("rbeta", [P, NG, T], F32)
        hnb = [kept("hnb%d" % k, [P, T, I], U8) for k in range(NK)]
        vfr = [kept("vfr%d" % k, [P, 2 * J], U8) for k in range(NK)]
        vfp = [[kept("vfp%d%d" % (k, g), [P, 2 * KP], U8) for g in range(NG)] for k in range(NK)]
        vfs = [kept("vfs%d" % g, [P, NK, KP], U8) for g in range(NG)]
        hfr = [[kept("hfr%d%d" % (k, h), [P, T, W], BF16) for h in range(NH)] for k in range(NK)]
        hnw = [[kept("hnw%d%d" % (k, h), [P, T, W], BF16) for h in range(NH)] for k in range(NK)]
        vnr = [[kept("vnr%d%d" % (g, k), [P, T, KP], BF16) for k in range(NK)] for g in range(NG)]
        vel = [[kept("vel%d%d" % (g, h), [P, T, KP], BF16) for h in range(NH)] for g in range(NG)]
        hfc = [[kept("hfc%d%d" % (k, h), [P, W], U32) for h in range(NH)] for k in range(NK)]
        hfs = [[kept("hfs%d%d" % (k, h), [P, W], U8) for h in range(NH)] for k in range(NK)]
        hnc = [[kept("hnc%d%d" % (k, h), [P, W], U32) for h in range(NH)] for k in range(NK)]
        hns = [[kept("hns%d%d" % (k, h), [P, W], U8) for h in range(NH)] for k in range(NK)]
        vnc = [[kept("vnc%d%d" % (g, k), [P, KP], U32) for k in range(NK)] for g in range(NG)]
        vns = [[kept("vns%d%d" % (g, k), [P, KP], U8) for k in range(NK)] for g in range(NG)]
        dc = [[kept("dc%d%d" % (g, h), [P, W], U32) for h in range(NH)] for g in range(NG)]
        ds = [[kept("ds%d%d" % (g, h), [P, W], U8) for h in range(NH)] for g in range(NG)]
        prw = kept("prw", [P, NG, 2 * L], U8)

        nc.vector.memset(vfs_raw[:].rearrange("p k n -> p (k n)").bitcast(I32), 0)
        nc.vector.memset(warm[:], 0.0)
        nc.gpsimd.memset(prs[:].rearrange("p g n -> p (g n)").bitcast(I32), 0)

        ctx.enter_context(tc.manual_schedule())

        hn_v = h_nudged_bytes.rearrange("(k p t) n -> k p t n", p=P, t=T)
        hf_v = h_free_neg.rearrange("(k p t) n -> k p t n", p=P, t=T)
        vn_v = v_nudged.rearrange("(k p t) n -> k p t n", p=P, t=T)
        vel_v = velocity.rearrange("(h a p) n -> h p a n", p=P, a=T)

        nc.scalar.dma_start(out=hsc[:], in_=h_nudged_scale.rearrange("(k p t) o -> p k (t o)", p=P, t=T))
        nc.scalar.dma_start(out=beta_sb[:], in_=beta.rearrange("(g p t) -> p g t", p=P, t=T))
        nc.scalar.activation(out=warm[:], in_=warm[:], func=COPY, scale=1.0)


        def ld(what, *ix):
            if what == "hf":
                k, h = ix
                nc.sync.dma_start(out=hfr[k][h][:], in_=hf_v[k][:, :, h * W:(h + 1) * W])
            elif what == "hn":
                nc.sync.dma_start(out=hnb[ix[0]][:], in_=hn_v[ix[0]])
            elif what == "vn":
                g, k = ix
                nc.sync.dma_start(out=vnr[g][k][:], in_=vn_v[k][:, :, g * KP:(g + 1) * KP])
            elif what == "vel":
                g, h = ix
                nc.sync.dma_start(out=vel[g][h][:], in_=vel_v[h][:, :, g * KP:(g + 1) * KP])
            elif what == "vfw":
                nc.sync.dma_start(out=vfr[ix[0]][:], in_=v_free_words[ix[0]])
            elif what == "prw":
                nc.sync.dma_start(out=prw[:], in_=proj_words.rearrange("g p n -> p g n"))
            else:
                dst, src = (vfs_raw, v_free_scales) if what == "vfs" else (prs, proj_scales)
                for q4 in range(T):
                    nc.sync.dma_start(
                        out=dst[32 * q4:32 * q4 + 4].bitcast(I32),
                        in_=src[:, 4 * q4:4 * q4 + 4, :].rearrange("g q n -> q g n").bitcast(I32),
                    )

        raws, codes, scales = {}, {}, {}
        for k in range(NK):
            for h in range(NH):
                raws["f", k, h], codes["f", k, h], scales["f", k, h] = hfr[k][h], hfc[k][h], hfs[k][h]
                raws["n", k, h], codes["n", k, h], scales["n", k, h] = hnw[k][h], hnc[k][h], hns[k][h]
            for g in range(NG):
                raws["v", g, k], codes["v", g, k], scales["v", g, k] = vnr[g][k], vnc[g][k], vns[g][k]

        def part(pt):
            return slice(0, W) if pt == 2 else slice(256 * pt, 256 * (pt + 1))

        def wid(k, h, pt, e):
            lo = part(pt).start
            hi = part(pt).stop
            for t in range(T):
                src = hnb[k][:, t, h * W + lo:h * W + hi].bitcast(FP8)
                if e == "S":
                    nc.scalar.activation(out=hnw[k][h][:, t, lo:hi], in_=src, func=COPY, scale=hsc[:, k, t:t + 1])
                else:
                    nc.vector.tensor_scalar(
                        out=hnw[k][h][:, t, lo:hi], in0=src, scalar1=hsc[:, k, t:t + 1], scalar2=None, op0=MULT)

        def copy_on(e, dst, src):
            if e == "V":
                nc.vector.tensor_copy(out=dst, in_=src)
            else:
                nc.scalar.copy(out=dst, in_=src)

        grouped = {}

        def new_grouped(key):
            if key not in grouped:
                grouped[key] = work.tile([P, W * T], BF16, name="grouped", tag="grouped", bufs=8, align_bytes=64)
            return grouped[key]

        def ilv(key, b, e):
            dst = new_grouped(key)[:, 1024 * b:1024 * (b + 1)]
            src = raws[key]
            if key[0] == "v":
                copy_on(
                    e,
                    dst.rearrange("p (t m j) -> p m j t", t=2, j=T),
                    src[:].rearrange("p j (m t) -> p m j t", t=T)[:, :, :, 2 * b:2 * b + 2],
                )
            else:
                copy_on(
                    e,
                    dst.rearrange("p (c i t) -> p c t i", i=4, t=T),
                    src[:, :, 256 * b:256 * (b + 1)].rearrange("p t (c i) -> p c t i", i=4),
                )

        def q(key, pt):
            s = part(pt)
            nc.vector.quantize_mx(
                out=codes[key][:, s].bitcast(FP8X4), scales=scales[key][:, s], in_=grouped[key][:, T * s.start:T * s.stop])

        def pw(k, g):
            nc.vector.tensor_copy(
                out=vfp[k][g][:].rearrange("p (t m b) -> p m t b", t=T, b=2),
                in_=vfr[k][:, 2 * KP * g:2 * KP * (g + 1)].rearrange("p (m t b) -> p m t b", t=T, b=2),
            )

        def ps(g):
            nc.vector.tensor_copy(
                out=vfs[g][:].rearrange("p k (t m) -> p k m t", t=T),
                in_=vfs_raw[:, :, KP * g:KP * (g + 1)].rearrange("p k (m t) -> p k m t", t=T),
            )

        def rb():
            nc.vector.reciprocal(out=rbeta[:].rearrange("p g t -> p (g t)"), in_=beta_sb[:].rearrange("p g t -> p (g t)"))

        acc, vts, cscs, dbfs, obs = {}, {}, {}, {}, {}

        def bank(b, shape, dtype):
            return psum.tile(shape, dtype, name="bank%d" % b, tag="bank%d" % b)

        def mm(g, h, t, s0, s1, b=None):
            if s0 == 0:
                acc[g, h, t] = bank(b, [P, W], F32)
            cols = slice(t * P, (t + 1) * P)
            for step in range(s0, s1):
                k = step % NK
                if step < NK:
                    lhsT, ls = vfp[k][g][:, 2 * t * P:2 * (t + 1) * P].bitcast(FP4X4), vfs[g][:, k, cols]
                    key = ("f", k, h)
                else:
                    lhsT, ls = vnc[g][k][:, cols].bitcast(FP8X4), vns[g][k][:, cols]
                    key = ("n", k, h)
                nc.tensor.matmul_mx(
                    out=acc[g, h, t][:], lhsT=lhsT, lhsT_scale=ls, rhs=codes[key][:].bitcast(FP8X4),
                    rhs_scale=scales[key][:], start=(step == 0), stop=(step == 2 * NK - 1))

        def vt(g, h, c, b):
            x = bank(b, [P, 256, 2], F32)
            vts[g, h, c] = x
            for i in range(2):
                words = vel[g][h][:, 2 * c + i, :].bitcast(F32)
                for u in range(2):
                    nc.tensor.transpose(x[:, i * P:(i + 1) * P, u], words[:, u:256:2], ident[:])

        def dr(g, h, t, e):
            if (g, h) not in cscs:
                cscs[g, h] = work.tile([P, T, W], F32, name="csc", tag="csc", bufs=2)
            dst, src, by = cscs[g, h][:, t, :], acc[g, h, t][:], rbeta[:, g, t:t + 1]
            if e == "S":
                nc.scalar.activation(out=dst, in_=src, func=COPY, scale=by)
            else:
                nc.vector.tensor_scalar(out=dst, in0=src, scalar1=by, scalar2=None, op0=MULT)

        def da(g, h, c):
            if (g, h) not in dbfs:
                dbfs[g, h] = work.tile([P, W * T], BF16, name="dbf", tag="dbf", bufs=2, align_bytes=64)
            nc.vector.tensor_tensor(
                out=dbfs[g, h][:, 1024 * c:1024 * (c + 1)].rearrange("p (x i t) -> p x t i", i=4, t=T),
                in0=cscs[g, h][:, :, 256 * c:256 * (c + 1)].rearrange("p t (x i) -> p x t i", i=4),
                in1=vts[g, h, c][:].bitcast(BF16).rearrange("p r t -> p (r t)").rearrange("p (x i t) -> p x t i", i=4, t=T),
                op=ADD,
            )

        def dq(g, h, c):
            s = part(c)
            nc.vector.quantize_mx(
                out=dc[g][h][:, s].bitcast(FP8X4), scales=ds[g][h][:, s], in_=dbfs[g, h][:, T * s.start:T * s.stop])

        def om(h, a, g0, g1, b=None):
            if g0 == 0:
                obs[h, a] = bank(b, [P, L], F32)
            cols = slice(a * P, (a + 1) * P)
            for g in range(g0, g1):
                nc.tensor.matmul_mx(
                    out=obs[h, a][:], lhsT=dc[g][h][:, cols].bitcast(FP8X4), lhsT_scale=ds[g][h][:, cols],
                    rhs=prw[:, g, :].bitcast(FP4X4), rhs_scale=prs[:, g, :], start=(g == 0), stop=(g == NG - 1))

        def st(h, a, e):
            x = work.tile([P, L], F32, name="res", tag="res", bufs=4)
            copy_on(e, x[:], obs[h, a][:])
            r = (h * T + a) * P
            nc.sync.dma_start(out=out[r:r + P, :], in_=x[:])

        ld("hn", 1)
        ld("hn", 0)
        ld("hf", 0, 0)
        ld("vfs")
        ld("hf", 1, 0)
        ld("vfw", 0)
        ld("vfw", 1)
        ld("vn", 0, 0)
        ld("vn", 0, 1)
        ld("vel", 0, 0)
        ld("hf", 0, 1)
        ld("hf", 1, 1)
        ld("vel", 0, 1)
        ld("vn", 1, 1)
        ld("vn", 1, 0)
        ld("vel", 2, 0)
        ld("vn", 2, 1)
        ld("vn", 2, 0)
        ld("vel", 1, 0)
        ld("vel", 1, 1)
        ld("prs")
        ld("vel", 2, 1)
        ld("prw")
        rb()
        wid(1, 1, 2, "V")
        wid(0, 1, 2, "V")
        wid(0, 0, 2, "V")
        wid(1, 0, 2, "S")
        ilv(("n", 1, 0), 1, "S")
        ilv(("f", 0, 0), 0, "S")
        ilv(("f", 0, 0), 1, "S")
        ilv(("n", 1, 0), 0, "V")
        ilv(("n", 0, 0), 0, "V")
        ilv(("n", 0, 0), 1, "V")
        ilv(("f", 1, 0), 0, "S")
        ilv(("f", 1, 0), 1, "S")
        ilv(("v", 0, 0), 1, "S")
        ilv(("v", 0, 1), 0, "S")
        ilv(("v", 0, 1), 1, "S")
        ilv(("f", 0, 1), 0, "S")
        ps(0)
        q(("f", 0, 0), 2)
        pw(0, 0)
        pw(1, 0)
        mm(0, 0, 3, 0, 1, 2)
        mm(0, 0, 1, 0, 1, 7)
        q(("n", 0, 0), 2)
        q(("f", 1, 0), 2)
        ilv(("v", 0, 0), 0, "V")
        q(("n", 1, 0), 2)
        q(("v", 0, 0), 2)
        q(("v", 0, 1), 0)
        mm(0, 0, 0, 0, 2, 5)
        mm(0, 0, 2, 0, 2, 0)
        ilv(("n", 0, 1), 1, "V")
        vt(0, 0, 1, 1)
        vt(0, 0, 0, 3)
        q(("v", 0, 1), 1)
        ilv(("f", 0, 1), 1, "V")
        ilv(("n", 0, 1), 0, "V")
        ilv(("f", 1, 1), 0, "V")
        mm(0, 0, 1, 1, 4)
        mm(0, 0, 3, 1, 4)
        mm(0, 0, 2, 2, 4)
        mm(0, 0, 0, 2, 4)
        ilv(("f", 1, 1), 1, "S")
        q(("f", 0, 1), 2)
        q(("f", 1, 1), 2)
        q(("n", 0, 1), 2)
        dr(0, 0, 1, "S")
        dr(0, 0, 2, "S")
        dr(0, 0, 0, "S")
        vt(0, 1, 0, 6)
        vt(0, 1, 1, 4)
        mm(0, 1, 0, 0, 1, 7)
        mm(0, 1, 3, 0, 2, 0)
        mm(0, 1, 1, 0, 3, 5)
        mm(0, 1, 3, 2, 3)
        mm(0, 1, 0, 1, 3)
        ilv(("n", 1, 1), 0, "V")
        pw(0, 1)
        ilv(("n", 1, 1), 1, "S")
        q(("n", 1, 1), 2)
        dr(0, 0, 3, "S")
        ps(1)
        mm(0, 1, 2, 0, 2, 2)
        mm(0, 1, 1, 3, 4)
        mm(0, 1, 3, 3, 4)
        mm(0, 1, 0, 3, 4)
        mm(0, 1, 2, 2, 4)
        ilv(("v", 1, 0), 0, "S")
        dr(0, 1, 1, "S")
        dr(0, 1, 3, "S")
        dr(0, 1, 2, "S")
        dr(0, 1, 0, "S")
        pw(1, 1)
        ilv(("v", 1, 1), 0, "V")
        q(("v", 1, 0), 0)
        q(("v", 1, 1), 0)
        mm(1, 1, 1, 0, 2, 5)
        mm(1, 0, 1, 0, 2, 0)
        mm(1, 0, 0, 0, 4, 2)
        mm(1, 1, 1, 2, 4)
        mm(1, 1, 0, 0, 4, 7)
        mm(1, 0, 1, 2, 4)
        da(0, 0, 1)
        da(0, 0, 0)
        ilv(("v", 1, 1), 1, "S")
        ilv(("v", 1, 0), 1, "S")
        q(("v", 1, 1), 1)
        q(("v", 1, 0), 1)
        mm(1, 1, 2, 0, 1, 1)
        mm(1, 0, 2, 0, 4, 3)
        da(0, 1, 0)
        dr(1, 1, 1, "S")
        dr(1, 1, 0, "S")
        ps(2)
        mm(1, 0, 3, 0, 4, 7)
        mm(1, 1, 2, 1, 4)
        mm(1, 1, 3, 0, 4, 5)
        ilv(("v", 2, 0), 0, "S")
        ilv(("v", 2, 1), 0, "S")
        vt(1, 0, 0, 6)
        da(0, 1, 1)
        dr(1, 1, 2, "S")
        dr(1, 0, 1, "S")
        dr(1, 0, 0, "S")
        dr(1, 1, 3, "S")
        q(("v", 2, 0), 0)
        vt(1, 0, 1, 1)
        vt(1, 1, 1, 0)
        vt(1, 1, 0, 2)
        pw(0, 2)
        dq(0, 0, 2)
        pw(1, 2)
        mm(2, 0, 1, 0, 1, 4)
        q(("v", 2, 1), 0)
        mm(2, 1, 0, 0, 4, 5)
        mm(2, 0, 1, 1, 4)
        da(1, 1, 0)
        ilv(("v", 2, 0), 1, "S")
        ilv(("v", 2, 1), 1, "S")
        dr(1, 0, 2, "S")
        dr(1, 0, 3, "S")
        mm(2, 1, 1, 0, 4, 2)
        q(("v", 2, 1), 1)
        q(("v", 2, 0), 1)
        da(1, 1, 1)
        dq(0, 1, 2)
        mm(2, 1, 3, 0, 4, 3)
        mm(2, 0, 2, 0, 4, 0)
        mm(2, 1, 2, 0, 4, 7)
        dr(2, 1, 3, "S")
        dr(2, 1, 1, "S")
        dr(2, 1, 2, "S")
        dr(2, 1, 0, "S")
        da(1, 0, 0)
        da(1, 0, 1)
        vt(2, 1, 0, 2)
        vt(2, 1, 1, 3)
        vt(2, 0, 0, 7)
        dq(1, 1, 2)
        dq(1, 0, 2)
        dr(2, 0, 1, "S")
        mm(2, 0, 0, 0, 4, 6)
        mm(2, 0, 3, 0, 4, 5)
        dr(2, 0, 0, "S")
        dr(2, 0, 3, "S")
        dr(2, 0, 2, "S")
        da(2, 1, 0)
        dq(2, 1, 0)
        om(1, 1, 0, 2, 6)
        om(1, 0, 0, 3, 4)
        om(1, 1, 2, 3)
        da(2, 1, 1)
        dq(2, 1, 1)
        om(1, 2, 0, 3, 2)
        da(2, 0, 0)
        st(1, 0, "S")
        st(1, 1, "S")
        st(1, 2, "S")
        dq(2, 0, 0)
        om(1, 3, 0, 3, 4)
        vt(2, 0, 1, 3)
        om(0, 0, 0, 3, 1)
        om(0, 1, 0, 3, 6)
        da(2, 0, 1)
        dq(2, 0, 1)
        om(0, 2, 0, 3, 3)
        st(1, 3, "S")
        st(0, 0, "S")
        st(0, 1, "V")
        st(0, 2, "S")
        om(0, 3, 0, 3, 1)
        st(0, 3, "V")
